import numpy as np
import ml_dtypes


def mxq(x, axis, fmt="e4m3"):
    dtype, down = {"e4m3": (ml_dtypes.float8_e4m3fn, 7), "e5m2": (ml_dtypes.float8_e5m2, 14)}[fmt]
    v = np.moveaxis(np.asarray(x, np.float32).astype(ml_dtypes.bfloat16).astype(np.float64), axis, -1)
    blocks = v.reshape(v.shape[:-1] + (-1, 32))
    amax = np.abs(blocks).max(-1, keepdims=True)
    byte = np.maximum(np.where(amax > 0, np.frexp(amax)[1] - 1 + 127, 0) - down, 1)
    scale = np.exp2(byte - 127.0)
    codes = (blocks / scale).astype(np.float32).astype(dtype).astype(np.float64)
    return np.moveaxis((codes * scale).reshape(v.shape), -1, axis)


WIDE = False


def mx_kscale(k):
    if not WIDE:
        return np.ones(k)
    levels = np.array([10, -10, 5, -5, 0])
    if k % 512:
        return np.exp2(np.random.permutation(np.resize(levels, k // 32))).repeat(32)
    a = np.empty((k // 512, 16))
    for p in range(k // 512):
        a[p, :8] = np.random.permutation(np.resize(levels, 8))
        for g in range(8):
            far = levels[np.abs(levels - a[p, g]) >= 10]
            a[p, g + 8] = far[np.random.randint(len(far))]
    return np.exp2(a.ravel()).repeat(32)


def f64(x):
    return np.asarray(x).astype(np.float64)


def striped8(idx):
    return np.asarray(idx).reshape(8, -1, 16).transpose(0, 2, 1).reshape(128, -1).astype(np.uint16)


def unstriped8(offs):
    return offs.reshape(8, 16, -1).transpose(0, 2, 1).reshape(8, -1).astype(np.int64)


def pick8(x, idx, run):
    r = np.arange(len(x))
    return x[r[:, None], idx[r % (8 * run) // run]]


E2M1 = np.array([0.0, 0.5, 1.0, 1.5, 2.0, 3.0, 4.0, 6.0, -0.0, -0.5, -1.0, -1.5, -2.0, -3.0, -4.0, -6.0])


def pack_weight(w, fmt):
    k, n = w.shape
    w = f64(np.asarray(w, np.float32).astype(ml_dtypes.bfloat16)).reshape(k // 32, 32, n)
    amax = np.abs(w).max(1)
    if fmt == "e4m3":
        byte = np.frexp(amax)[1] - 1 + 127 - 7
    else:
        mant, ex = np.frexp(amax / 6.0)
        byte = np.where(mant > 0.5, ex, ex - 1) + 127
    byte = np.clip(np.where(amax > 0, byte, 1), 1, 254)
    scaled = (w * np.exp2(127.0 - byte)[:, None, :]).reshape(k, n).astype(np.float32)
    by_word = np.ascontiguousarray(scaled.reshape(k // 512, 128, 4, n).transpose(0, 1, 3, 2))
    if fmt == "e4m3":
        words = by_word.astype(ml_dtypes.float8_e4m3fn).view(np.uint8)
    else:
        c = by_word.astype(ml_dtypes.float4_e2m1fn).view(np.uint8) & 0xF
        words = (c[..., 0::2] | (c[..., 1::2] << 4)).reshape(k // 512, 128, 2 * n)
    return np.ascontiguousarray(words), np.ascontiguousarray(byte.astype(np.uint8).reshape(k // 512, 16, n))


def unpack_weight(words, scales, fmt):
    g, _, n = scales.shape
    words = np.ascontiguousarray(words).reshape(g, 128, n, -1)
    if fmt == "e4m3":
        vals = words.view(ml_dtypes.float8_e4m3fn).astype(np.float64)
    else:
        nib = np.empty((g, 128, n, 4), np.uint8)
        nib[..., 0::2] = words & 0xF
        nib[..., 1::2] = words >> 4
        vals = E2M1[nib]
    vals = vals * np.repeat(np.exp2(scales.astype(np.float64) - 127.0), 8, axis=1)[..., None]
    return vals.transpose(0, 1, 3, 2).reshape(g * 512, n)


D, V, Q, I = 512, 2048, 128, 512


def setup_inputs():
    n = np.random.standard_normal
    idx = np.stack([np.random.permutation(V)[:I] for _ in range(8)])
    fd = mx_kscale(D)
    vocp = pack_weight(n((D, V)) / fd[:, None], "e2m1")
    return {
        "hid": (n((D, Q)) * 1.0 / np.sqrt(D) * fd[:, None]).astype(np.float32),
        "voc_words": vocp[0],
        "voc_scales": vocp[1],
        "sw": (np.random.uniform(0.5, 2.0, (1, I))).astype(np.float32),
        "old": (0.5 * n((Q, V))).astype(np.float32),
        "offs": striped8(idx),
    }


def reference(hid, voc_words, voc_scales, sw, old, offs):
    idx = unstriped8(offs)
    vocu = unpack_weight(voc_words, voc_scales, "e2m1")
    hidq = mxq(f64(hid), 0, "e4m3")
    a = hidq.T @ vocu
    m1 = np.max(a, axis=1, keepdims=True)
    px = np.exp(pick8(a, idx, 16) - m1)
    zl = np.sum(px, axis=1, keepdims=True)
    dzl = np.sum(f64(sw) / (px / zl + 0.001) * px / np.square(zl) * (-1.0), axis=1, keepdims=True)
    dpx = f64(sw) / (px / zl + 0.001) / zl + dzl
    e1 = dpx * px
    s1 = np.zeros((Q, V))
    s1[np.arange(Q)[:, None], idx[np.arange(Q) % 128 // 16]] = e1
    y = s1 + f64(old)
    return y

@@ -1,0 +1,157 @@
+import math
+from contextlib import ExitStack
+
+import concourse.mybir as mybir
+from concourse.masks import make_identity
+
+D, V, Q, I = 512, 2048, 128, 512
+FLOPS = 2 * D * V * Q
+
+F32 = mybir.dt.float32
+BF16 = mybir.dt.bfloat16
+I32 = mybir.dt.int32
+U32 = mybir.dt.uint32
+U16 = mybir.dt.uint16
+U8 = mybir.dt.uint8
+FP8X4 = mybir.dt.float8_e4m3fn_x4
+FP4X4 = mybir.dt.float4_e2m1fn_x4
+ALU = mybir.AluOpType
+ACT = mybir.ActivationFunctionType
+
+P = 128
+PACK = 4
+EPS = 0.001
+SCORE_PIECES = (256, 256, 512, 512, 512)
+STORE_PIECES = (256, 512, 512, 512, 256)
+LOG_TERMS = 8
+BITS_SLOPE = math.log(2.0) / 2.0**23
+BITS_SHIFT = 88.0
+
+
+def tile_attend_blistshare_heads_kernel(tc, hid, voc_words, voc_scales, sw, old, offs, out):
+    nc = tc.nc
+    with ExitStack() as ctx:
+        sb = ctx.enter_context(tc.tile_pool(name="sb", bufs=1))
+        ps = ctx.enter_context(tc.psum_pool(name="ps", bufs=1))
+
+        offsets = sb.tile([P, I // 16], U16, name="offsets")
+        hid_raw = sb.tile([P, PACK, Q], F32, name="hid_raw", tag="staged")
+        words = sb.tile([P, 2 * V], U8, name="words", align_bytes=64)
+        voc_plane = sb.tile([P, V], U8, name="voc_plane", align_bytes=64)
+        sw_cols = sb.tile([P, PACK], F32, name="sw_cols")
+
+        nc.vector.memset(voc_plane[:].bitcast(I32), 0)
+        nc.sync.dma_start(hid_raw[:], hid.rearrange("(p j) q -> p j q", j=PACK))
+        nc.sync.dma_start(words[:].bitcast(I32), voc_words[0].bitcast(I32))
+        for quad in range(4):
+            nc.scalar.dma_start(
+                voc_plane[32 * quad : 32 * quad + 4, :].bitcast(I32),
+                voc_scales[0, 4 * quad : 4 * quad + 4, :].bitcast(I32),
+            )
+        nc.sync.dma_start(sw_cols[:], sw.rearrange("o (p c) -> (o p) c", c=PACK))
+        nc.sync.dma_start(offsets[:], offs)
+
+        scattered = sb.tile([P, V], F32, name="scattered")
+        nc.vector.memset(scattered[:], 0.0)
+
+        ident = sb.tile([P, P], F32, name="ident")
+        make_identity(nc, ident[:])
+        series = sb.tile([P, 16], F32, name="series")
+        for t in range(LOG_TERMS):
+            k = LOG_TERMS - t
+            nc.gpsimd.memset(series[:, t : t + 1], 0.5 * (-1.0) ** k / k)
+        shift = sb.tile([P, 1], F32, name="shift")
+        nc.gpsimd.memset(shift[:], BITS_SHIFT)
+
+        sw_bank = ps.tile([P, PACK, P], F32, name="sw_bank")
+        for c in range(PACK):
+            nc.tensor.transpose(sw_bank[:, c, :], sw_cols[:, c : c + 1].to_broadcast([P, P]), ident[:])
+        half_sw = sb.tile([P, I], F32, name="half_sw")
+        nc.scalar.activation(
+            half_sw[:].rearrange("p (n c) -> p n c", c=PACK),
+            sw_bank[:].rearrange("p c n -> p n c"),
+            ACT.Copy,
+            scale=0.5,
+        )
+
+        grouped = sb.tile([P, Q, PACK], BF16, name="grouped", align_bytes=64)
+        nc.vector.tensor_copy(
+            grouped[:].rearrange("p (c i) j -> p c j i", i=4),
+            hid_raw[:].rearrange("p j (c i) -> p c j i", i=4),
+        )
+        hid_codes = sb.tile([P, Q], U32, name="hid_codes", align_bytes=64)
+        hid_plane = sb.tile([P, Q], U8, name="hid_plane", align_bytes=64)
+        nc.vector.quantize_mx(
+            out=hid_codes[:].bitcast(FP8X4),
+            scales=hid_plane[:],
+            in_=grouped[:].rearrange("p q j -> p (q j)"),
+        )
+
+        old_sb = sb.tile([P, V], F32, name="old_sb", tag="staged")
+        nc.sync.dma_start(old_sb[:], old)
+
+        scores = sb.tile([P, V], F32, name="scores")
+        piece_max = sb.tile([P, len(SCORE_PIECES)], F32, name="piece_max")
+        v0 = 0
+        for n, width in enumerate(SCORE_PIECES):
+            bank = ps.tile([P, width], F32, name="bank%d" % n)
+            nc.tensor.matmul_mx(
+                out=bank[:],
+                lhsT=hid_codes[:].bitcast(FP8X4),
+                lhsT_scale=hid_plane[:],
+                rhs=words[:, 2 * v0 : 2 * (v0 + width)].bitcast(FP4X4),
+                rhs_scale=voc_plane[:, v0 : v0 + width],
+                start=True,
+                stop=True,
+            )
+            nc.vector.tensor_scalar(
+                scores[:, v0 : v0 + width], bank[:], 1.0, None, ALU.mult, ALU.max,
+                accum_out=piece_max[:, n : n + 1],
+            )
+            v0 = v0 + width
+        neg_max = sb.tile([P, 1], F32, name="neg_max")
+        nc.vector.tensor_reduce(neg_max[:], piece_max[:], mybir.AxisListType.X, ALU.max, negate=True)
+
+        px = sb.tile([P, I], F32, name="px")
+        zl = sb.tile([P, 1], F32, name="zl")
+        picked = sb.tile([P, I], F32, name="picked")
+        nc.vector.tensor_copy(picked[:], scores[:].indirect(offsets[:]))
+        nc.scalar.activation(px[:], picked[:], ACT.Exp, bias=neg_max[:], scale=1.0, accum_out=zl[:])
+
+        base = sb.tile([P, 1], F32, name="base")
+        nc.vector.tensor_scalar(
+            base[:], neg_max[:], 0.5, 0.5 * (BITS_SHIFT - math.log(EPS)), ALU.mult, ALU.add
+        )
+        guess_inv = sb.tile([P, 1], F32, name="guess_inv")
+        nc.scalar.activation(guess_inv[:], zl[:].bitcast(U32), ACT.Exp, bias=shift[:], scale=-BITS_SLOPE)
+        nc.vector.tensor_scalar(
+            series[:, LOG_TERMS : LOG_TERMS + 1], zl[:].bitcast(I32), -0.5 * BITS_SLOPE, base[:], ALU.mult, ALU.add
+        )
+        rest = sb.tile([P, 1], F32, name="rest")
+        nc.vector.tensor_scalar(rest[:], guess_inv[:], zl[:], -1.0, ALU.mult, ALU.add)
+        horner = sb.tile([P, LOG_TERMS + 1], F32, name="horner")
+        nc.vector.tensor_tensor_scan(
+            horner[:], rest[:].to_broadcast([P, LOG_TERMS + 1]), series[:, 0 : LOG_TERMS + 1], 0.0, ALU.mult, ALU.add
+        )
+        th = sb.tile([P, I], F32, name="th")
+        nc.scalar.activation(th[:], picked[:], ACT.Tanh, bias=horner[:, LOG_TERMS : LOG_TERMS + 1], scale=0.5)
+
+        inv_zl = sb.tile([P, 1], F32, name="inv_zl")
+        nc.vector.reciprocal(inv_zl[:], zl[:])
+        neg_inv_zl = sb.tile([P, 1], F32, name="neg_inv_zl")
+        nc.vector.tensor_scalar(neg_inv_zl[:], inv_zl[:], -1.0, None, ALU.mult)
+
+        g = sb.tile([P, I], F32, name="g")
+        g_sum = sb.tile([P, 1], F32, name="g_sum")
+        nc.vector.scalar_tensor_tensor(g[:], th[:], 1.0, half_sw[:], ALU.add, ALU.mult, accum_out=g_sum[:])
+        h = sb.tile([P, I], F32, name="h")
+        nc.vector.tensor_scalar(h[:], px[:], neg_inv_zl[:], g_sum[:], ALU.mult, ALU.mult)
+        nc.vector.tensor_tensor(scattered[:].indirect(offsets[:]), g[:], h[:], ALU.add)
+
+        v0 = 0
+        for n, width in enumerate(STORE_PIECES):
+            total = sb.tile([P, width], F32, name="total%d" % n)
+            nc.vector.tensor_tensor(total[:], scattered[:, v0 : v0 + width], old_sb[:, v0 : v0 + width], ALU.add)
+            queue = nc.sync if n % 2 == 0 else nc.scalar
+            queue.dma_start(out[:, v0 : v0 + width], total[:])
+            v0 = v0 + width

@@ -21,9 +21,9 @@ ACT = mybir.ActivationFunctionType
 P = 128
 PACK = 4
 EPS = 0.001
-SCORE_PIECES = (256, 256, 512, 512, 512)
+WORD_LOADS = ((256, 512), (256, 512, 512))
 STORE_PIECES = (256, 512, 512, 512, 256)
-LOG_TERMS = 8
+LOG_TERMS = 16
 BITS_SLOPE = math.log(2.0) / 2.0**23
 BITS_SHIFT = 88.0
 
@@ -35,46 +35,41 @@ def tile_attend_blistshare_heads_kernel(tc, hid, voc_words, voc_scales, sw, old,
         ps = ctx.enter_context(tc.psum_pool(name="ps", bufs=1))
 
         offsets = sb.tile([P, I // 16], U16, name="offsets")
-        hid_raw = sb.tile([P, PACK, Q], F32, name="hid_raw", tag="staged")
-        words = sb.tile([P, 2 * V], U8, name="words", align_bytes=64)
+        hid_raw = sb.tile([P, PACK, Q], F32, name="hid_raw", tag="after_cast")
         voc_plane = sb.tile([P, V], U8, name="voc_plane", align_bytes=64)
-        sw_cols = sb.tile([P, PACK], F32, name="sw_cols")
 
         nc.vector.memset(voc_plane[:].bitcast(I32), 0)
+        minus_one = sb.tile([P, LOG_TERMS], F32, name="minus_one", tag="after_series", align_bytes=64)
+        nc.vector.memset(minus_one[:], -1.0)
+        twice_k = sb.tile([P, LOG_TERMS], F32, name="twice_k")
+        nc.vector.tensor_tensor_scan(
+            twice_k[:], minus_one[:], minus_one[:], 2.0 * LOG_TERMS + 2.0, ALU.add, ALU.add
+        )
+        series = sb.tile([P, LOG_TERMS + 1], F32, name="series")
+        nc.vector.reciprocal(series[:, 0:LOG_TERMS], twice_k[:])
+        nc.vector.tensor_scalar(series[:, 1:LOG_TERMS:2], series[:, 1:LOG_TERMS:2], -1.0, None, ALU.mult)
+
+        span0, span1 = sum(WORD_LOADS[0]), sum(WORD_LOADS[1])
+        words0 = sb.tile([P, 2 * span0], U8, name="words0", align_bytes=64)
+        words1 = sb.tile([P, 2 * span1], U8, name="words1", tag="after_series", align_bytes=64)
+        word_tiles = (words0, words1)
         nc.sync.dma_start(hid_raw[:], hid.rearrange("(p j) q -> p j q", j=PACK))
-        nc.sync.dma_start(words[:].bitcast(I32), voc_words[0].bitcast(I32))
+        nc.sync.dma_start(words0[:].bitcast(I32), voc_words[0, :, 0 : 2 * span0].bitcast(I32))
         for quad in range(4):
-            nc.scalar.dma_start(
+            queue = nc.sync if quad % 2 == 0 else nc.scalar
+            queue.dma_start(
                 voc_plane[32 * quad : 32 * quad + 4, :].bitcast(I32),
                 voc_scales[0, 4 * quad : 4 * quad + 4, :].bitcast(I32),
             )
-        nc.sync.dma_start(sw_cols[:], sw.rearrange("o (p c) -> (o p) c", c=PACK))
+        nc.sync.dma_start(words1[:].bitcast(I32), voc_words[0, :, 2 * span0 : 2 * V].bitcast(I32))
         nc.sync.dma_start(offsets[:], offs)
-
-        scattered = sb.tile([P, V], F32, name="scattered")
-        nc.vector.memset(scattered[:], 0.0)
 
         ident = sb.tile([P, P], F32, name="ident")
         make_identity(nc, ident[:])
-        series = sb.tile([P, 16], F32, name="series")
-        for t in range(LOG_TERMS):
-            k = LOG_TERMS - t
-            nc.gpsimd.memset(series[:, t : t + 1], 0.5 * (-1.0) ** k / k)
         shift = sb.tile([P, 1], F32, name="shift")
         nc.gpsimd.memset(shift[:], BITS_SHIFT)
 
-        sw_bank = ps.tile([P, PACK, P], F32, name="sw_bank")
-        for c in range(PACK):
-            nc.tensor.transpose(sw_bank[:, c, :], sw_cols[:, c : c + 1].to_broadcast([P, P]), ident[:])
-        half_sw = sb.tile([P, I], F32, name="half_sw")
-        nc.scalar.activation(
-            half_sw[:].rearrange("p (n c) -> p n c", c=PACK),
-            sw_bank[:].rearrange("p c n -> p n c"),
-            ACT.Copy,
-            scale=0.5,
-        )
-
-        grouped = sb.tile([P, Q, PACK], BF16, name="grouped", align_bytes=64)
+        grouped = sb.tile([P, Q, PACK], BF16, name="grouped", tag="after_quantise", align_bytes=64)
         nc.vector.tensor_copy(
             grouped[:].rearrange("p (c i) j -> p c j i", i=4),
             hid_raw[:].rearrange("p j (c i) -> p c j i", i=4),
@@ -87,28 +82,44 @@ def tile_attend_blistshare_heads_kernel(tc, hid, voc_words, voc_scales, sw, old,
             in_=grouped[:].rearrange("p q j -> p (q j)"),
         )
 
-        old_sb = sb.tile([P, V], F32, name="old_sb", tag="staged")
+        sw_cols = sb.tile([P, PACK], F32, name="sw_cols", tag="after_cast")
+        nc.sync.dma_start(sw_cols[:], sw.rearrange("o (p c) -> (o p) c", c=PACK))
+        half_sw = sb.tile([P, PACK], F32, name="half_sw")
+        nc.scalar.activation(half_sw[:], sw_cols[:], ACT.Copy, scale=0.5)
+        old_sb = sb.tile([P, V], F32, name="old_sb", tag="after_cast")
         nc.sync.dma_start(old_sb[:], old)
+        scattered = sb.tile([P, V], F32, name="scattered", tag="after_quantise", align_bytes=64)
+        nc.gpsimd.memset(scattered[:], 0.0)
 
         scores = sb.tile([P, V], F32, name="scores")
-        piece_max = sb.tile([P, len(SCORE_PIECES)], F32, name="piece_max")
+        piece_max = sb.tile([P, sum(len(pieces) for pieces in WORD_LOADS)], F32, name="piece_max")
         v0 = 0
-        for n, width in enumerate(SCORE_PIECES):
-            bank = ps.tile([P, width], F32, name="bank%d" % n)
-            nc.tensor.matmul_mx(
-                out=bank[:],
-                lhsT=hid_codes[:].bitcast(FP8X4),
-                lhsT_scale=hid_plane[:],
-                rhs=words[:, 2 * v0 : 2 * (v0 + width)].bitcast(FP4X4),
-                rhs_scale=voc_plane[:, v0 : v0 + width],
-                start=True,
-                stop=True,
-            )
-            nc.vector.tensor_scalar(
-                scores[:, v0 : v0 + width], bank[:], 1.0, None, ALU.mult, ALU.max,
-                accum_out=piece_max[:, n : n + 1],
-            )
-            v0 = v0 + width
+        n = 0
+        for words, pieces in zip(word_tiles, WORD_LOADS):
+            c0 = 0
+            for width in pieces:
+                bank = ps.tile([P, width], F32, name="bank%d" % n, tag="bank%d" % n)
+                nc.tensor.matmul_mx(
+                    out=bank[:],
+                    lhsT=hid_codes[:].bitcast(FP8X4),
+                    lhsT_scale=hid_plane[:],
+                    rhs=words[:, 2 * c0 : 2 * (c0 + width)].bitcast(FP4X4),
+                    rhs_scale=voc_plane[:, v0 : v0 + width],
+                    start=True,
+                    stop=True,
+                )
+                nc.vector.tensor_scalar(
+                    scores[:, v0 : v0 + width], bank[:], 1.0, None, ALU.mult, ALU.max,
+                    accum_out=piece_max[:, n : n + 1],
+                )
+                v0 = v0 + width
+                c0 = c0 + width
+                n = n + 1
+
+        sw_bank = ps.tile([P, PACK, P], F32, name="sw_bank", tag="bank%d" % (n - 1))
+        for c in range(PACK):
+            nc.tensor.transpose(sw_bank[:, c, :], half_sw[:, c : c + 1].to_broadcast([P, P]), ident[:])
+
         neg_max = sb.tile([P, 1], F32, name="neg_max")
         nc.vector.tensor_reduce(neg_max[:], piece_max[:], mybir.AxisListType.X, ALU.max, negate=True)
 
@@ -131,7 +142,7 @@ def tile_attend_blistshare_heads_kernel(tc, hid, voc_words, voc_scales, sw, old,
         nc.vector.tensor_scalar(rest[:], guess_inv[:], zl[:], -1.0, ALU.mult, ALU.add)
         horner = sb.tile([P, LOG_TERMS + 1], F32, name="horner")
         nc.vector.tensor_tensor_scan(
-            horner[:], rest[:].to_broadcast([P, LOG_TERMS + 1]), series[:, 0 : LOG_TERMS + 1], 0.0, ALU.mult, ALU.add
+            horner[:], rest[:].to_broadcast([P, LOG_TERMS + 1]), series[:], 0.0, ALU.mult, ALU.add
         )
         th = sb.tile([P, I], F32, name="th")
         nc.scalar.activation(th[:], picked[:], ACT.Tanh, bias=horner[:, LOG_TERMS : LOG_TERMS + 1], scale=0.5)
@@ -143,7 +154,15 @@ def tile_attend_blistshare_heads_kernel(tc, hid, voc_words, voc_scales, sw, old,
 
         g = sb.tile([P, I], F32, name="g")
         g_sum = sb.tile([P, 1], F32, name="g_sum")
-        nc.vector.scalar_tensor_tensor(g[:], th[:], 1.0, half_sw[:], ALU.add, ALU.mult, accum_out=g_sum[:])
+        nc.vector.scalar_tensor_tensor(
+            g[:].rearrange("p (n c) -> p n c", c=PACK),
+            th[:].rearrange("p (n c) -> p n c", c=PACK),
+            1.0,
+            sw_bank[:].rearrange("p c n -> p n c"),
+            ALU.add,
+            ALU.mult,
+            accum_out=g_sum[:],
+        )
         h = sb.tile([P, I], F32, name="h")
         nc.vector.tensor_scalar(h[:], px[:], neg_inv_zl[:], g_sum[:], ALU.mult, ALU.mult)
         nc.vector.tensor_tensor(scattered[:].indirect(offsets[:]), g[:], h[:], ALU.add)

@@ -58,8 +58,8 @@ def tile_attend_blistshare_heads_kernel(tc, hid, voc_words, voc_scales, sw, old,
         for quad in range(4):
             queue = nc.sync if quad % 2 == 0 else nc.scalar
             queue.dma_start(
-                voc_plane[32 * quad : 32 * quad + 4, :].bitcast(I32),
-                voc_scales[0, 4 * quad : 4 * quad + 4, :].bitcast(I32),
+                voc_plane[quad : P : 32, :].bitcast(I32),
+                voc_scales[0, quad : 16 : 4, :].bitcast(I32),
             )
         nc.sync.dma_start(words1[:].bitcast(I32), voc_words[0, :, 2 * span0 : 2 * V].bitcast(I32))
         nc.sync.dma_start(offsets[:], offs)
@@ -69,7 +69,7 @@ def tile_attend_blistshare_heads_kernel(tc, hid, voc_words, voc_scales, sw, old,
         shift = sb.tile([P, 1], F32, name="shift")
         nc.gpsimd.memset(shift[:], BITS_SHIFT)
 
-        grouped = sb.tile([P, Q, PACK], BF16, name="grouped", tag="after_quantise", align_bytes=64)
+        grouped = sb.tile([P, Q, PACK], BF16, name="grouped", align_bytes=64)
         nc.vector.tensor_copy(
             grouped[:].rearrange("p (c i) j -> p c j i", i=4),
             hid_raw[:].rearrange("p j (c i) -> p c j i", i=4),
@@ -83,15 +83,14 @@ def tile_attend_blistshare_heads_kernel(tc, hid, voc_words, voc_scales, sw, old,
         )
 
         sw_cols = sb.tile([P, PACK], F32, name="sw_cols", tag="after_cast")
-        nc.sync.dma_start(sw_cols[:], sw.rearrange("o (p c) -> (o p) c", c=PACK))
+        with nc.allow_non_contiguous_dma(reason="one weight to a partition and column"):
+            nc.sync.dma_start(sw_cols[:], sw.rearrange("o (c p) -> p (o c)", p=P))
         half_sw = sb.tile([P, PACK], F32, name="half_sw")
         nc.scalar.activation(half_sw[:], sw_cols[:], ACT.Copy, scale=0.5)
         old_sb = sb.tile([P, V], F32, name="old_sb", tag="after_cast")
         nc.sync.dma_start(old_sb[:], old)
-        scattered = sb.tile([P, V], F32, name="scattered", tag="after_quantise", align_bytes=64)
-        nc.gpsimd.memset(scattered[:], 0.0)
 
-        scores = sb.tile([P, V], F32, name="scores")
+        scores = sb.tile([P, V], F32, name="scores", tag="window")
         piece_max = sb.tile([P, sum(len(pieces) for pieces in WORD_LOADS)], F32, name="piece_max")
         v0 = 0
         n = 0
@@ -129,6 +128,9 @@ def tile_attend_blistshare_heads_kernel(tc, hid, voc_words, voc_scales, sw, old,
         nc.vector.tensor_copy(picked[:], scores[:].indirect(offsets[:]))
         nc.scalar.activation(px[:], picked[:], ACT.Exp, bias=neg_max[:], scale=1.0, accum_out=zl[:])
 
+        scattered = sb.tile([P, V], F32, name="scattered", tag="window")
+        nc.gpsimd.memset(scattered[:], 0.0)
+
         base = sb.tile([P, 1], F32, name="base")
         nc.vector.tensor_scalar(
             base[:], neg_max[:], 0.5, 0.5 * (BITS_SHIFT - math.log(EPS)), ALU.mult, ALU.add
@@ -155,13 +157,7 @@ def tile_attend_blistshare_heads_kernel(tc, hid, voc_words, voc_scales, sw, old,
         g = sb.tile([P, I], F32, name="g")
         g_sum = sb.tile([P, 1], F32, name="g_sum")
         nc.vector.scalar_tensor_tensor(
-            g[:].rearrange("p (n c) -> p n c", c=PACK),
-            th[:].rearrange("p (n c) -> p n c", c=PACK),
-            1.0,
-            sw_bank[:].rearrange("p c n -> p n c"),
-            ALU.add,
-            ALU.mult,
-            accum_out=g_sum[:],
+            g[:], th[:], 1.0, sw_bank[:].rearrange("p c n -> p (c n)"), ALU.add, ALU.mult, accum_out=g_sum[:]
         )
         h = sb.tile([P, I], F32, name="h")
         nc.vector.tensor_scalar(h[:], px[:], neg_inv_zl[:], g_sum[:], ALU.mult, ALU.mult)

import math
from contextlib import ExitStack

import concourse.mybir as mybir
from concourse.masks import make_identity

D, V, Q, I = 512, 2048, 128, 512
FLOPS = 2 * D * V * Q

F32 = mybir.dt.float32
BF16 = mybir.dt.bfloat16
I32 = mybir.dt.int32
U32 = mybir.dt.uint32
U16 = mybir.dt.uint16
U8 = mybir.dt.uint8
FP8X4 = mybir.dt.float8_e4m3fn_x4
FP4X4 = mybir.dt.float4_e2m1fn_x4
ALU = mybir.AluOpType
ACT = mybir.ActivationFunctionType

P = 128
PACK = 4
EPS = 0.001
WORD_LOADS = ((256, 512), (256, 512, 512))
STORE_PIECES = (256, 512, 512, 512, 256)
LOG_TERMS = 16
BITS_SLOPE = math.log(2.0) / 2.0**23
BITS_SHIFT = 88.0


def tile_attend_blistshare_heads_kernel(tc, hid, voc_words, voc_scales, sw, old, offs, out):
    nc = tc.nc
    with ExitStack() as ctx:
        sb = ctx.enter_context(tc.tile_pool(name="sb", bufs=1))
        ps = ctx.enter_context(tc.psum_pool(name="ps", bufs=1))

        offsets = sb.tile([P, I // 16], U16, name="offsets")
        hid_raw = sb.tile([P, PACK, Q], F32, name="hid_raw", tag="after_cast")
        voc_plane = sb.tile([P, V], U8, name="voc_plane", align_bytes=64)

        nc.vector.memset(voc_plane[:].bitcast(I32), 0)
        minus_one = sb.tile([P, LOG_TERMS], F32, name="minus_one", tag="after_series", align_bytes=64)
        nc.vector.memset(minus_one[:], -1.0)
        twice_k = sb.tile([P, LOG_TERMS], F32, name="twice_k")
        nc.vector.tensor_tensor_scan(
            twice_k[:], minus_one[:], minus_one[:], 2.0 * LOG_TERMS + 2.0, ALU.add, ALU.add
        )
        series = sb.tile([P, LOG_TERMS + 1], F32, name="series")
        nc.vector.reciprocal(series[:, 0:LOG_TERMS], twice_k[:])
        nc.vector.tensor_scalar(series[:, 1:LOG_TERMS:2], series[:, 1:LOG_TERMS:2], -1.0, None, ALU.mult)

        span0, span1 = sum(WORD_LOADS[0]), sum(WORD_LOADS[1])
        words0 = sb.tile([P, 2 * span0], U8, name="words0", align_bytes=64)
        words1 = sb.tile([P, 2 * span1], U8, name="words1", tag="after_series", align_bytes=64)
        word_tiles = (words0, words1)
        nc.sync.dma_start(hid_raw[:], hid.rearrange("(p j) q -> p j q", j=PACK))
        nc.sync.dma_start(words0[:].bitcast(I32), voc_words[0, :, 0 : 2 * span0].bitcast(I32))
        for quad in range(4):
            queue = nc.sync if quad % 2 == 0 else nc.scalar
            queue.dma_start(
                voc_plane[quad : P : 32, :].bitcast(I32),
                voc_scales[0, quad : 16 : 4, :].bitcast(I32),
            )
        nc.sync.dma_start(words1[:].bitcast(I32), voc_words[0, :, 2 * span0 : 2 * V].bitcast(I32))
        nc.sync.dma_start(offsets[:], offs)

        ident = sb.tile([P, P], F32, name="ident")
        make_identity(nc, ident[:])
        shift = sb.tile([P, 1], F32, name="shift")
        nc.gpsimd.memset(shift[:], BITS_SHIFT)

        grouped = sb.tile([P, Q, PACK], BF16, name="grouped", align_bytes=64)
        nc.vector.tensor_copy(
            grouped[:].rearrange("p (c i) j -> p c j i", i=4),
            hid_raw[:].rearrange("p j (c i) -> p c j i", i=4),
        )
        hid_codes = sb.tile([P, Q], U32, name="hid_codes", align_bytes=64)
        hid_plane = sb.tile([P, Q], U8, name="hid_plane", align_bytes=64)
        nc.vector.quantize_mx(
            out=hid_codes[:].bitcast(FP8X4),
            scales=hid_plane[:],
            in_=grouped[:].rearrange("p q j -> p (q j)"),
        )

        sw_cols = sb.tile([P, PACK], F32, name="sw_cols", tag="after_cast")
        with nc.allow_non_contiguous_dma(reason="one weight to a partition and column"):
            nc.sync.dma_start(sw_cols[:], sw.rearrange("o (c p) -> p (o c)", p=P))
        half_sw = sb.tile([P, PACK], F32, name="half_sw")
        nc.scalar.activation(half_sw[:], sw_cols[:], ACT.Copy, scale=0.5)
        old_sb = sb.tile([P, V], F32, name="old_sb", tag="after_cast")
        nc.sync.dma_start(old_sb[:], old)

        scores = sb.tile([P, V], F32, name="scores", tag="window")
        piece_max = sb.tile([P, sum(len(pieces) for pieces in WORD_LOADS)], F32, name="piece_max")
        v0 = 0
        n = 0
        for words, pieces in zip(word_tiles, WORD_LOADS):
            c0 = 0
            for width in pieces:
                bank = ps.tile([P, width], F32, name="bank%d" % n, tag="bank%d" % n)
                nc.tensor.matmul_mx(
                    out=bank[:],
                    lhsT=hid_codes[:].bitcast(FP8X4),
                    lhsT_scale=hid_plane[:],
                    rhs=words[:, 2 * c0 : 2 * (c0 + width)].bitcast(FP4X4),
                    rhs_scale=voc_plane[:, v0 : v0 + width],
                    start=True,
                    stop=True,
                )
                nc.vector.tensor_scalar(
                    scores[:, v0 : v0 + width], bank[:], 1.0, None, ALU.mult, ALU.max,
                    accum_out=piece_max[:, n : n + 1],
                )
                v0 = v0 + width
                c0 = c0 + width
                n = n + 1

        sw_bank = ps.tile([P, PACK, P], F32, name="sw_bank", tag="bank%d" % (n - 1))
        for c in range(PACK):
            nc.tensor.transpose(sw_bank[:, c, :], half_sw[:, c : c + 1].to_broadcast([P, P]), ident[:])

        neg_max = sb.tile([P, 1], F32, name="neg_max")
        nc.vector.tensor_reduce(neg_max[:], piece_max[:], mybir.AxisListType.X, ALU.max, negate=True)

        px = sb.tile([P, I], F32, name="px")
        zl = sb.tile([P, 1], F32, name="zl")
        picked = sb.tile([P, I], F32, name="picked")
        nc.vector.tensor_copy(picked[:], scores[:].indirect(offsets[:]))
        nc.scalar.activation(px[:], picked[:], ACT.Exp, bias=neg_max[:], scale=1.0, accum_out=zl[:])

        scattered = sb.tile([P, V], F32, name="scattered", tag="window")
        nc.gpsimd.memset(scattered[:], 0.0)

        base = sb.tile([P, 1], F32, name="base")
        nc.vector.tensor_scalar(
            base[:], neg_max[:], 0.5, 0.5 * (BITS_SHIFT - math.log(EPS)), ALU.mult, ALU.add
        )
        guess_inv = sb.tile([P, 1], F32, name="guess_inv")
        nc.scalar.activation(guess_inv[:], zl[:].bitcast(U32), ACT.Exp, bias=shift[:], scale=-BITS_SLOPE)
        nc.vector.tensor_scalar(
            series[:, LOG_TERMS : LOG_TERMS + 1], zl[:].bitcast(I32), -0.5 * BITS_SLOPE, base[:], ALU.mult, ALU.add
        )
        rest = sb.tile([P, 1], F32, name="rest")
        nc.vector.tensor_scalar(rest[:], guess_inv[:], zl[:], -1.0, ALU.mult, ALU.add)
        horner = sb.tile([P, LOG_TERMS + 1], F32, name="horner")
        nc.vector.tensor_tensor_scan(
            horner[:], rest[:].to_broadcast([P, LOG_TERMS + 1]), series[:], 0.0, ALU.mult, ALU.add
        )
        th = sb.tile([P, I], F32, name="th")
        nc.scalar.activation(th[:], picked[:], ACT.Tanh, bias=horner[:, LOG_TERMS : LOG_TERMS + 1], scale=0.5)

        inv_zl = sb.tile([P, 1], F32, name="inv_zl")
        nc.vector.reciprocal(inv_zl[:], zl[:])
        neg_inv_zl = sb.tile([P, 1], F32, name="neg_inv_zl")
        nc.vector.tensor_scalar(neg_inv_zl[:], inv_zl[:], -1.0, None, ALU.mult)

        g = sb.tile([P, I], F32, name="g")
        g_sum = sb.tile([P, 1], F32, name="g_sum")
        nc.vector.scalar_tensor_tensor(
            g[:], th[:], 1.0, sw_bank[:].rearrange("p c n -> p (c n)"), ALU.add, ALU.mult, accum_out=g_sum[:]
        )
        h = sb.tile([P, I], F32, name="h")
        nc.vector.tensor_scalar(h[:], px[:], neg_inv_zl[:], g_sum[:], ALU.mult, ALU.mult)
        nc.vector.tensor_tensor(scattered[:].indirect(offsets[:]), g[:], h[:], ALU.add)

        v0 = 0
        for n, width in enumerate(STORE_PIECES):
            total = sb.tile([P, width], F32, name="total%d" % n)
            nc.vector.tensor_tensor(total[:], scattered[:, v0 : v0 + width], old_sb[:, v0 : v0 + width], ALU.add)
            queue = nc.sync if n % 2 == 0 else nc.scalar
            queue.dma_start(out[:, v0 : v0 + width], total[:])
            v0 = v0 + width
